import numpy as np, ml_dtypes
CORES = [5,29,101,125,133,157,229,253]
N = 8
import mx_ref
BF = ml_dtypes.bfloat16
def entries(a):
    return np.ascontiguousarray(a.T).reshape(-1)
def table(e):
    return np.ascontiguousarray(np.reshape(e, (-1, 16)).T).astype(np.int32)
def f(rng, *shape):
    return mx_ref.flush((rng.standard_normal(shape, dtype=np.float32) * np.exp2(rng.integers(-2, 3, shape[:-1] + (1,)))).astype(BF))
def wide(rng, *shape, cols=0):
    v = rng.standard_normal(shape, dtype=np.float32) * np.exp2(rng.integers(-12, 13, shape)).astype(np.float32)
    if cols: v *= np.repeat(np.exp2(rng.integers(-cols, cols + 1, shape[:-2] + (1, shape[-1] // 4))) * (rng.random(shape[:-2] + (1, shape[-1] // 4)) > 0.0625), 4, axis=-1).astype(np.float32)
    return mx_ref.flush(v.astype(BF))
NL, LO, O = 1024, 128, 2
HOST = np.array([0 if k < 128 else 1 for k in CORES])
def tables_of(s):
    return np.stack([table(e) for e in s])
def won(rng, win):
    v = rng.integers(1, 2 ** rng.integers(0, 21, NL) + 1)
    s = rng.integers(0, v, (N, NL)); s[win, np.arange(NL)] = v
    return tables_of(s)
def setup_inputs(rng):
    s = rng.integers(0, 2 ** rng.integers(0, 21, NL) + 1, (N, NL))
    return {"x": f(rng, N, 128, 4 * NL), "w": f(rng, N, 128, 512 * O), "sc": tables_of(s)}
def setup_inputs_ties(rng):
    s = np.zeros((N, NL), int)
    for q in range(N):
        for i, j in enumerate(rng.permutation(LO) + q * LO):
            a, b = [rng.permutation(np.flatnonzero(HOST == h)) for h in rng.permutation(2)]
            if i % 3 == 0: e = np.arange(N)
            elif i % 3 == 1: e = a[:rng.integers(2, len(a) + 1)]
            else: e = np.concatenate([a[:rng.integers(1, len(a) + 1)], b[:rng.integers(1, len(b) + 1)]])
            v = 0 if i == 0 else 2 ** 20 if i < 4 else int(rng.integers(1, 2 ** 20 + 1))
            s[:, j] = rng.integers(0, max(v, 1), N); s[e, j] = v
    return {**setup_inputs(rng), "sc": tables_of(s)}
def setup_inputs_close(rng):
    v = rng.integers(1, 2 ** rng.integers(0, 21, NL) + 1)
    v.reshape(N, LO)[:, rng.permutation(LO)[:2]] = [1, 2 ** 20]
    win = rng.integers(0, N, NL); second = (win + rng.integers(1, N, NL)) % N
    s = np.where(rng.random((N, NL)) < 0.5, v - 1, rng.integers(0, v, (N, NL)))
    s[second, np.arange(NL)] = v - 1; s[win, np.arange(NL)] = v
    return {**setup_inputs(rng), "sc": tables_of(s)}
def setup_inputs_most(rng):
    p = int(rng.integers(0, N))
    win = (p + rng.integers(1, N, (N, LO))) % N
    for i, q in enumerate(rng.permutation(N)):
        if i == 0: win[q] = p
        elif i > 1: win[q, rng.permutation(LO)[:-(-9 * LO // 10)]] = p
    return {**setup_inputs(rng), "sc": won(rng, win.reshape(-1))}
def setup_inputs_sides(rng):
    win = np.zeros((N, LO), int)
    for h in range(2):
        own = rng.permutation(np.flatnonzero(HOST == h))
        for i, q in enumerate(own):
            win[q] = rng.choice(np.flatnonzero(HOST == (1 - h if i < len(own) // 2 else h)), LO)
    return {**setup_inputs(rng), "sc": won(rng, win.reshape(-1))}
def setup_inputs_spread(rng):
    d = setup_inputs(rng); d["x"] = wide(rng, N, 128, 4 * NL, cols=6); return d
def check_inputs(d):
    b = []
    for r in range(N):
        s = entries(d["sc"][r])
        if s.min() < 0 or s.max() > 2 ** 20: b.append("sc")
    return b
def reference(x, w, sc):
    best = np.stack([entries(e) for e in sc]).argmax(axis=0)
    y = np.zeros((N, 128, O * LO), np.float32)
    for q in range(N):
        M = np.concatenate([x[best[l]][:, 4 * l:4 * l + 4] for l in range(q * LO, q * LO + LO)], axis=1)
        M = mx_ref.quantize(M)
        for o in range(O): y[q][:, LO * o:LO * o + LO] = mx_ref.matmul(mx_ref.quantize(w[q][:, 512 * o:512 * o + 512]), M)
    return {"y": y}

@@ -1,0 +1,232 @@
+from concourse.bass import DstId, RemoteDMATransfer
+from concourse.mybir import dt, AluOpType, ActivationFunctionType
+
+N, NL, LO, O = 8, 1024, 128, 2
+KC = LO // 16
+
+SCRATCH = {
+    "xb": ("sbuf", [128, 4 * NL], "bfloat16"),
+    "wb": ("sbuf", [128, 512 * O], "bfloat16"),
+    "sck": ("sbuf", [128, NL // 16], "int32"),
+    "kin": ("sbuf", [128, KC * N], "int32"),
+    "kin8": ("sbuf", [128, KC * N], "int32"),
+    "slot": ("sbuf", [128, KC * N], "int32"),
+    "m0": ("sbuf", [128, KC * N], "int32"),
+    "m1": ("sbuf", [128, KC * 4], "int32"),
+    "m2": ("sbuf", [128, KC * 2], "int32"),
+    "m3": ("sbuf", [128, KC], "int32"),
+    "m4": ("sbuf", [128, KC], "int32"),
+    "m5": ("sbuf", [128, KC], "float32"),
+    "ip": ("sbuf", [128, KC], "int32"),
+    "ic": ("sbuf", [128, KC], "int32"),
+    "jp": ("sbuf", [128, KC], "int32"),
+    "jt": ("sbuf", [128, KC], "int32"),
+    "jf": ("sbuf", [128, KC], "float32"),
+    "off": ("sbuf", [128, KC], "uint16"),
+    "sq": ("sbuf", [128, NL], "float8_e4m3fn_x4"),
+    "ss": ("sbuf", [128, NL], "uint8"),
+    "rk": ("sbuf", [128, KC], "int32"),
+    "rq": ("sbuf", [128, LO], "float8_e4m3fn_x4"),
+    "rs": ("sbuf", [128, LO], "uint8"),
+    "winq": ("sbuf", [128, NL], "float8_e4m3fn_x4"),
+    "wins": ("sbuf", [128, NL], "uint8"),
+    "mq": ("sbuf", [128, LO], "float8_e4m3fn_x4"),
+    "ms": ("sbuf", [128, LO], "uint8"),
+    "wq": ("sbuf", [128, LO * O], "float8_e4m3fn_x4"),
+    "ws": ("sbuf", [128, LO * O], "uint8"),
+    "ps0": ("psum", [128, 512], "float32"),
+    "ps1": ("psum", [128, 512], "float32"),
+    "ysb": ("sbuf", [128, LO * O], "float32"),
+}
+SEMAPHORES = (["lsc", "lw", "kown", "iot", "jv", "qg0", "qg1", "qo", "qw", "am", "offs", "pc", "pscale",
+               "mm0", "mm1", "cp0", "cp1", "st0", "st1", "arrk", "arrq", "arrs", "rak", "raq", "ras", "left"]
+              + ["lx%d" % i for i in range(N)])
+
+
+def mask_of(engines):
+    return sum(1 << e for e in engines)
+
+
+def plan(r, cores, topo):
+    me = cores[r]
+    plane = [q for q in range(N) if q == r or topo.same_plane(me, cores[q])]
+    cross = [q for q in range(N) if q not in plane]
+    i, n = plane.index(r), len(plane)
+    ports = [c for c in topo.cores_of(me) if c != me and all(topo.may_write(c, cores[q]) for q in cross)]
+    ports.sort(key=lambda c: (topo.die(c) != topo.die(me), c))
+    far = [c for c in topo.cores_of(me) if c != me and c not in ports and topo.die(c) != topo.die(me)]
+    relays = {q: ports[(i + k) % len(ports)] for k, q in enumerate(cross)}
+    via = plane[(i + 1) % n]
+    relays[via] = far[0]
+    direct = [plane[(i + 2) % n], plane[(i + 3) % n]]
+    groups = [cross, [via] + direct]
+    out = topo.engines(me, cores[direct[0]])
+    on = topo.engines(me, far[0])
+    f, h = len(on) // 4, len(out) // 2
+    cols = {q: on[f * k:f * k + f] for k, q in enumerate(cross)}
+    cols.update({via: [e for e in on if e not in out], direct[0]: out[:h], direct[1]: out[h:]})
+    keys = {direct[0]: out[0:2], direct[1]: out[2:4]}
+    rest = [e for e in on if e not in out[0:4]]
+    for k, q in enumerate(cross + [via]):
+        keys[q] = rest[2 * k:2 * k + 2]
+    return {"groups": groups, "order": groups[0] + groups[1] + [r], "relays": relays, "keys": keys, "cols": cols}
+
+
+def relay_program(g, core, T, topo, r, q):
+    S = T.sem
+    dst = T.cores[q]
+    rid, pid = topo.addr(dst, core)
+    mask = topo.mask(core, dst)
+    p = plan(r, T.cores, topo)
+    slot = LO * (N - 1 - r)
+    g.wait_ge(S.rak, len(p["keys"][q]))
+    g.remote_dma(T.kin[:, KC * r:KC * r + KC], T.rk[:, :], S.arrk, S.left, pid, rid, mask)
+    g.wait_ge(S.raq, len(p["cols"][q]))
+    g.remote_dma(T.winq[:, slot:slot + LO].bitcast(dt.uint8), T.rq[:, 0:LO].bitcast(dt.uint8), S.arrq, S.left,
+                 pid, rid, mask)
+    g.wait_ge(S.ras, len(p["cols"][q]))
+    g.remote_dma(T.wins[:, slot:slot + LO], T.rs[:, 0:LO], S.arrs, S.left, pid, rid, mask)
+    g.wait_ge(S.left, 3 * len(topo.engines(core, dst)))
+
+
+def rank_program(g, core, T, topo):
+    S = T.sem
+    rank = T.rank_of(core)
+    if rank is None:
+        for r in range(N):
+            for q, c in plan(r, T.cores, topo)["relays"].items():
+                if c == core:
+                    relay_program(g, core, T, topo, r, q)
+        return
+
+    p = plan(rank, T.cores, topo)
+    order = p["order"]
+    sy, sc, v, te = g.sync, g.scalar, g.vector, g.tensor
+
+    two = (sy, sc)
+    for h in range(8):
+        two[h % 2].dma_start(T.sck[16 * h:16 * h + 16, :], T.sc[:, :]).then_inc(S.lsc, 16)
+    for i, q in enumerate(order):
+        two[i % 2].dma_start(T.xb[:, 512 * i:512 * i + 512], T.x[:, 512 * q:512 * q + 512]).then_inc(S["lx%d" % i], 16)
+    sy.wait_ge(S["lx%d" % (N - 2)], 16)
+    sy.dma_start(T.wb[:, :], T.w[:, :]).then_inc(S.lw, 16)
+
+    g.iota(T.ip[:, :], [[0, KC]], 0, 1).then_inc(S.iot, 1)
+    g.iota(T.ic[:, :], [[16, KC]], 0, 0).then_inc(S.iot, 1)
+    g.iota(T.slot[:, :], [[-1, N], [0, KC]], N - 1, 0).then_inc(S.iot, 1)
+    v.wait_ge(S.iot, 3)
+    v.tensor_scalar(T.jp[:, :], T.ip[:, :], 15, None, AluOpType.bitwise_and).then_inc(S.jv, 1)
+    v.wait_ge(S.jv, 1)
+    v.tensor_tensor(T.jt[:, :], T.jp[:, :], T.ic[:, :], AluOpType.add).then_inc(S.jv, 1)
+    v.wait_ge(S.jv, 2)
+    v.tensor_scalar(T.jf[:, :], T.jt[:, :], 1.0 / LO, None, AluOpType.mult).then_inc(S.jv, 1)
+
+    def quant(i, oq, os, sem):
+        v.wait_ge(S["lx%d" % i], 16)
+        v.quantize_mx(oq, os, T.xb[:, 512 * i:512 * i + 512]).then_inc(sem, 1)
+
+    i = 0
+    for n, group in enumerate(p["groups"]):
+        for q in group:
+            quant(i, T.sq[:, LO * i:LO * i + LO], T.ss[:, LO * i:LO * i + LO], S["qg%d" % n])
+            i += 1
+    v.wait_ge(S.lsc, 16 * 8)
+    v.tensor_copy(T.kin[:, KC * rank:KC * rank + KC], T.sck[:, KC * rank:KC * rank + KC]).then_inc(S.kown, 1)
+    mine = LO * (N - 1 - rank)
+    quant(N - 1, T.winq[:, mine:mine + LO], T.wins[:, mine:mine + LO], S.qo)
+
+    left = [0]
+
+    def send(kind, qs):
+        out = []
+        for q in qs:
+            i = order.index(q)
+            far = q in p["relays"]
+            dst = p["relays"][q] if far else T.cores[q]
+            if kind == "k":
+                src = T.sck[:, KC * q:KC * q + KC]
+                to = T.rk[:, :] if far else T.kin[:, KC * rank:KC * rank + KC]
+                rsem = S.rak if far else S.arrk
+            elif kind == "q":
+                src = T.sq[:, LO * i:LO * i + LO].bitcast(dt.uint8)
+                to = (T.rq[:, 0:LO] if far else T.winq[:, mine:mine + LO]).bitcast(dt.uint8)
+                rsem = S.raq if far else S.arrq
+            else:
+                src = T.ss[:, LO * i:LO * i + LO]
+                to = T.rs[:, 0:LO] if far else T.wins[:, mine:mine + LO]
+                rsem = S.ras if far else S.arrs
+            e = p["keys" if kind == "k" else "cols"][q]
+            rid, pid = topo.addr(dst, core)
+            out.append(RemoteDMATransfer(dst_ids=[DstId(rid=rid, pnc=pid)], dma_engine_mask=mask_of(e),
+                                         remote_sem=rsem, src=src, dst=to))
+            left[0] += len(e)
+        g.remote_dma_fused(out, local_sem=S.left)
+
+    g.wait_ge(S.lsc, 16 * 8)
+    send("k", order[:N - 1])
+    for n, group in enumerate(p["groups"]):
+        g.wait_ge(S["qg%d" % n], len(group))
+        send("q", group)
+        send("s", group)
+
+    nk = nc = 0
+    for r in range(N):
+        if r == rank:
+            continue
+        pr = plan(r, T.cores, topo)
+        if rank in pr["relays"]:
+            e = len(topo.engines(pr["relays"][rank], core))
+            nk, nc = nk + e, nc + e
+        else:
+            nk, nc = nk + len(pr["keys"][rank]), nc + len(pr["cols"][rank])
+
+    v.wait_ge(S.arrk, nk)
+    v.wait_ge(S.kown, 1)
+    v.tensor_scalar(T.kin8[:, :], T.kin[:, :], N, None, AluOpType.mult).then_inc(S.am, 1)
+    v.wait_ge(S.am, 1)
+    v.tensor_tensor(T.m0[:, :], T.kin8[:, :], T.slot[:, :], AluOpType.add).then_inc(S.am, 1)
+    v.wait_ge(S.am, 2)
+    v.tensor_tensor(T.m1[:, :], T.m0[:, 0:4 * KC], T.m0[:, 4 * KC:8 * KC], AluOpType.max).then_inc(S.am, 1)
+    v.wait_ge(S.am, 3)
+    v.tensor_tensor(T.m2[:, :], T.m1[:, 0:2 * KC], T.m1[:, 2 * KC:4 * KC], AluOpType.max).then_inc(S.am, 1)
+    v.wait_ge(S.am, 4)
+    v.tensor_tensor(T.m3[:, :], T.m2[:, 0:KC], T.m2[:, KC:2 * KC], AluOpType.max).then_inc(S.am, 1)
+    v.wait_ge(S.am, 5)
+    v.tensor_scalar(T.m4[:, :], T.m3[:, :], N - 1, None, AluOpType.bitwise_and).then_inc(S.am, 1)
+    v.wait_ge(S.am, 6)
+    v.wait_ge(S.jv, 3)
+    v.tensor_tensor(T.m5[:, :], T.m4[:, :], T.jf[:, :], AluOpType.add).then_inc(S.am, 1)
+    v.wait_ge(S.am, 7)
+    v.tensor_scalar(T.off[:, :], T.m5[:, :], float(LO), None, AluOpType.mult).then_inc(S.offs, 1)
+
+    v.wait_ge(S.lw, 16)
+    v.quantize_mx(T.wq[:, :], T.ws[:, :], T.wb[:, :]).then_inc(S.qw, 1)
+
+    v.wait_ge(S.offs, 1)
+    v.wait_ge(S.qo, 1)
+    v.wait_ge(S.arrq, nc)
+    v.tensor_copy(T.mq[:, 0:LO].bitcast(dt.uint32),
+                  T.winq[:, 0:NL].bitcast(dt.uint32).indirect(T.off[:, 0:KC])).then_inc(S.pc, 1)
+    sc.wait_ge(S.offs, 1)
+    sc.wait_ge(S.qo, 1)
+    sc.wait_ge(S.arrs, nc)
+    sc.activation(T.ms[:, 0:LO], T.wins[:, 0:NL].indirect(T.off[:, 0:KC]),
+                  ActivationFunctionType.Copy).then_inc(S.pscale, 1)
+
+    te.wait_ge(S.qw, 1)
+    te.wait_ge(S.pc, 1)
+    te.wait_ge(S.pscale, 1)
+    for o, (ps, mm) in enumerate(((T.ps0, S.mm0), (T.ps1, S.mm1))):
+        te.matmul_mx(ps[:, 0:LO], T.wq[:, LO * o:LO * o + LO], T.ws[:, LO * o:LO * o + LO], T.mq[:, 0:LO],
+                     T.ms[:, 0:LO], True, True).then_inc(mm, 1)
+    v.wait_ge(S.mm0, 1)
+    v.tensor_copy(T.ysb[:, 0:LO], T.ps0[:, 0:LO]).then_inc(S.cp0, 1)
+    sc.wait_ge(S.mm1, 1)
+    sc.activation(T.ysb[:, LO:2 * LO], T.ps1[:, 0:LO], ActivationFunctionType.Copy).then_inc(S.cp1, 1)
+    sy.wait_ge(S.cp0, 1)
+    sy.dma_start(T.y[:, 0:LO], T.ysb[:, 0:LO]).then_inc(S.st0, 16)
+    sc.wait_ge(S.cp1, 1)
+    sc.dma_start(T.y[:, LO:2 * LO], T.ysb[:, LO:2 * LO]).then_inc(S.st1, 16)
+    sy.wait_ge(S.st0, 16)
+    sc.wait_ge(S.st1, 16)
+    g.wait_ge(S.left, left[0])

@@ -1,33 +1,29 @@
 from concourse.bass import DstId, RemoteDMATransfer
-from concourse.mybir import dt, AluOpType, ActivationFunctionType
+from concourse.mybir import dt, AluOpType, AxisListType, ActivationFunctionType
 
 N, NL, LO, O = 8, 1024, 128, 2
 KC = LO // 16
+H = N // 2
+KP = 32
 
 SCRATCH = {
     "xb": ("sbuf", [128, 4 * NL], "bfloat16"),
     "wb": ("sbuf", [128, 512 * O], "bfloat16"),
-    "sck": ("sbuf", [128, NL // 16], "int32"),
+    "sck": ("sbuf", [128, KC * N], "int32"),
     "kin": ("sbuf", [128, KC * N], "int32"),
-    "kin8": ("sbuf", [128, KC * N], "int32"),
-    "slot": ("sbuf", [128, KC * N], "int32"),
-    "m0": ("sbuf", [128, KC * N], "int32"),
-    "m1": ("sbuf", [128, KC * 4], "int32"),
-    "m2": ("sbuf", [128, KC * 2], "int32"),
+    "key": ("sbuf", [128, KC * N], "float32"),
     "m3": ("sbuf", [128, KC], "int32"),
     "m4": ("sbuf", [128, KC], "int32"),
-    "m5": ("sbuf", [128, KC], "float32"),
     "ip": ("sbuf", [128, KC], "int32"),
     "ic": ("sbuf", [128, KC], "int32"),
     "jp": ("sbuf", [128, KC], "int32"),
-    "jt": ("sbuf", [128, KC], "int32"),
-    "jf": ("sbuf", [128, KC], "float32"),
+    "jt": ("sbuf", [128, KC], "float32"),
     "off": ("sbuf", [128, KC], "uint16"),
     "sq": ("sbuf", [128, NL], "float8_e4m3fn_x4"),
     "ss": ("sbuf", [128, NL], "uint8"),
     "rk": ("sbuf", [128, KC], "int32"),
-    "rq": ("sbuf", [128, LO], "float8_e4m3fn_x4"),
-    "rs": ("sbuf", [128, LO], "uint8"),
+    "rq": ("sbuf", [128, 2 * LO], "float8_e4m3fn_x4"),
+    "rs": ("sbuf", [128, 4 * LO], "uint8"),
     "winq": ("sbuf", [128, NL], "float8_e4m3fn_x4"),
     "wins": ("sbuf", [128, NL], "uint8"),
     "mq": ("sbuf", [128, LO], "float8_e4m3fn_x4"),
@@ -38,55 +34,92 @@ SCRATCH = {
     "ps1": ("psum", [128, 512], "float32"),
     "ysb": ("sbuf", [128, LO * O], "float32"),
 }
-SEMAPHORES = (["lsc", "lw", "kown", "iot", "jv", "qg0", "qg1", "qo", "qw", "am", "offs", "pc", "pscale",
-               "mm0", "mm1", "cp0", "cp1", "st0", "st1", "arrk", "arrq", "arrs", "rak", "raq", "ras", "left"]
-              + ["lx%d" % i for i in range(N)])
+SEMAPHORES = (["lsc", "keys", "fill", "lw0", "lw1", "arrp", "iot", "jv", "qo", "qw0", "qw1", "am", "offs", "pc",
+               "pscale", "mm0", "mm1", "cp0", "cp1", "st0", "st1", "arrk", "arrl", "arrq", "arrs", "left"]
+              + ["lx%d" % i for i in range(N)] + ["qc%d" % i for i in range(N)] + ["ra%d" % i for i in range(4)])
 
 
 def mask_of(engines):
     return sum(1 << e for e in engines)
 
 
+def deal(engines, n):
+    k = len(engines) // n
+    return [engines[k * i:k * i + k] for i in range(n)]
+
+
 def plan(r, cores, topo):
     me = cores[r]
+    chip = [c for c in topo.cores_of(me) if c != me]
     plane = [q for q in range(N) if q == r or topo.same_plane(me, cores[q])]
     cross = [q for q in range(N) if q not in plane]
-    i, n = plane.index(r), len(plane)
-    ports = [c for c in topo.cores_of(me) if c != me and all(topo.may_write(c, cores[q]) for q in cross)]
-    ports.sort(key=lambda c: (topo.die(c) != topo.die(me), c))
-    far = [c for c in topo.cores_of(me) if c != me and c not in ports and topo.die(c) != topo.die(me)]
-    relays = {q: ports[(i + k) % len(ports)] for k, q in enumerate(cross)}
-    via = plane[(i + 1) % n]
-    relays[via] = far[0]
-    direct = [plane[(i + 2) % n], plane[(i + 3) % n]]
-    groups = [cross, [via] + direct]
-    out = topo.engines(me, cores[direct[0]])
-    on = topo.engines(me, far[0])
-    f, h = len(on) // 4, len(out) // 2
-    cols = {q: on[f * k:f * k + f] for k, q in enumerate(cross)}
-    cols.update({via: [e for e in on if e not in out], direct[0]: out[:h], direct[1]: out[h:]})
-    keys = {direct[0]: out[0:2], direct[1]: out[2:4]}
-    rest = [e for e in on if e not in out[0:4]]
-    for k, q in enumerate(cross + [via]):
-        keys[q] = rest[2 * k:2 * k + 2]
-    return {"groups": groups, "order": groups[0] + groups[1] + [r], "relays": relays, "keys": keys, "cols": cols}
+    i = plane.index(r)
+    ports = [c for c in chip if all(topo.may_write(c, cores[q]) for q in cross)]
+    near = [c for c in ports if topo.die(c) == topo.die(me)]
+    far = [c for c in ports if c not in near]
+    helper = [c for c in chip if c not in ports and topo.die(c) != topo.die(me)][0]
+    pairs = [(t, t + H) for t in sorted({q % H for q in cross})]
+    partner = (r + H) % N
+    via = plane[(i + 1) % len(plane)]
+    other = (via + H) % N
+    out = topo.engines(me, cores[partner])
+    on = topo.engines(me, helper)
+    stay = [e for e in on if e not in out]
+    beside = [c for c in chip if c not in ports and topo.die(c) == topo.die(me)][0]
+    ports = near + far
+
+    to = {q: ports[(i + k) % len(ports)] for k, q in enumerate(cross)}
+    to.update({via: helper, other: beside, partner: cores[partner]})
+    cross = sorted(cross, key=lambda q: to[q] in far)
+
+    def hops(kind, owners, lanes):
+        return [(kind, (q,), to[q], e) for q, e in zip(owners, lanes)]
+
+    calls = [hops("k", cross, deal(on, 4)),
+             hops("k", [via, other, partner], deal(stay, 2) + [out]),
+             hops("q", [partner] + cross, deal(out, 2)[:1] + deal(out, 4)[2:] + deal(stay, 2)),
+             hops("s", [partner, via, other] + cross, deal(out, 2)[:1] + deal(out, 4)[2:] + deal(stay, 4)),
+             hops("q", [other, via], deal(stay, 2))]
+    return {"order": [partner] + cross + [via, other, r], "sides": (sorted(cross), plane), "calls": calls}
 
 
-def relay_program(g, core, T, topo, r, q):
-    S = T.sem
-    dst = T.cores[q]
+def transfer(topo, core, dst, engines, sem, src, to):
     rid, pid = topo.addr(dst, core)
-    mask = topo.mask(core, dst)
-    p = plan(r, T.cores, topo)
-    slot = LO * (N - 1 - r)
-    g.wait_ge(S.rak, len(p["keys"][q]))
-    g.remote_dma(T.kin[:, KC * r:KC * r + KC], T.rk[:, :], S.arrk, S.left, pid, rid, mask)
-    g.wait_ge(S.raq, len(p["cols"][q]))
-    g.remote_dma(T.winq[:, slot:slot + LO].bitcast(dt.uint8), T.rq[:, 0:LO].bitcast(dt.uint8), S.arrq, S.left,
-                 pid, rid, mask)
-    g.wait_ge(S.ras, len(p["cols"][q]))
-    g.remote_dma(T.wins[:, slot:slot + LO], T.rs[:, 0:LO], S.arrs, S.left, pid, rid, mask)
-    g.wait_ge(S.left, 3 * len(topo.engines(core, dst)))
+    return RemoteDMATransfer(dst_ids=[DstId(rid=rid, pnc=pid)], dma_engine_mask=mask_of(engines), remote_sem=sem,
+                             src=src, dst=to)
+
+
+def piece(T, names, kind, a, n):
+    buf = T[names["kqs".index(kind)]]
+    if kind == "k":
+        return buf[:, KC * a:KC * a + KC]
+    view = buf[:, LO * a:LO * (a + n)]
+    return view.bitcast(dt.uint8) if kind == "q" else view
+
+
+def landing(T, topo, kind, r, q):
+    if kind != "k":
+        return piece(T, ("kin", "winq", "wins"), kind, N - 1 - r, 1), "arr" + kind
+    sem = "arrp" if r % H == q % H else "arrl" if topo.same_plane(T.cores[r], T.cores[q]) else "arrk"
+    return piece(T, ("kin",), kind, r, 1), sem
+
+
+def steps(p, core):
+    return [hop for call in p["calls"] for hop in call if hop[2] == core]
+
+
+def relay_program(g, core, T, topo, r, p):
+    S = T.sem
+    left = 0
+    for n, (kind, owners, _, engines) in enumerate(steps(p, core)):
+        g.wait_ge(S["ra%d" % n], len(engines))
+        out = topo.engines(core, T.cores[owners[0]])
+        to, sem = landing(T, topo, kind, r, owners[0])
+        g.remote_dma_fused([transfer(topo, core, T.cores[owners[0]], out, S[sem],
+                                     piece(T, ("rk", "rq", "rs"), kind, 0, 1), to)], local_sem=S.left)
+        left += len(out)
+    if left:
+        g.wait_ge(S.left, left)
 
 
 def rank_program(g, core, T, topo):
@@ -94,9 +127,7 @@ def rank_program(g, core, T, topo):
     rank = T.rank_of(core)
     if rank is None:
         for r in range(N):
-            for q, c in plan(r, T.cores, topo)["relays"].items():
-                if c == core:
-                    relay_program(g, core, T, topo, r, q)
+            relay_program(g, core, T, topo, r, plan(r, T.cores, topo))
         return
 
     p = plan(rank, T.cores, topo)
@@ -104,119 +135,111 @@ def rank_program(g, core, T, topo):
     sy, sc, v, te = g.sync, g.scalar, g.vector, g.tensor
 
     two = (sy, sc)
-    for h in range(8):
-        two[h % 2].dma_start(T.sck[16 * h:16 * h + 16, :], T.sc[:, :]).then_inc(S.lsc, 16)
+    for h in range(2):
+        two[h].dma_start(T.sck[16 * h:16 * h + 16, :], T.sc[:, :]).then_inc(S.lsc, 16)
     for i, q in enumerate(order):
         two[i % 2].dma_start(T.xb[:, 512 * i:512 * i + 512], T.x[:, 512 * q:512 * q + 512]).then_inc(S["lx%d" % i], 16)
     sy.wait_ge(S["lx%d" % (N - 2)], 16)
-    sy.dma_start(T.wb[:, :], T.w[:, :]).then_inc(S.lw, 16)
+    for o in range(O):
+        sy.dma_start(T.wb[:, 512 * o:512 * o + 512], T.w[:, 512 * o:512 * o + 512]).then_inc(S["lw%d" % o], 16)
 
     g.iota(T.ip[:, :], [[0, KC]], 0, 1).then_inc(S.iot, 1)
     g.iota(T.ic[:, :], [[16, KC]], 0, 0).then_inc(S.iot, 1)
-    g.iota(T.slot[:, :], [[-1, N], [0, KC]], N - 1, 0).then_inc(S.iot, 1)
-    v.wait_ge(S.iot, 3)
-    v.tensor_scalar(T.jp[:, :], T.ip[:, :], 15, None, AluOpType.bitwise_and).then_inc(S.jv, 1)
-    v.wait_ge(S.jv, 1)
-    v.tensor_tensor(T.jt[:, :], T.jp[:, :], T.ic[:, :], AluOpType.add).then_inc(S.jv, 1)
-    v.wait_ge(S.jv, 2)
-    v.tensor_scalar(T.jf[:, :], T.jt[:, :], 1.0 / LO, None, AluOpType.mult).then_inc(S.jv, 1)
+
+    v.memset(T.sck[32:64, :], 0).then_inc(S.fill, 1)
+    v.memset(T.sck[64:128, :], 0).then_inc(S.fill, 1)
+
+    def keys(scores, r):
+        v.tensor_scalar(T.key[0:KP, KC * r:KC * r + KC], scores, N, N - 1 - r,
+                        AluOpType.mult, AluOpType.add).then_inc(S.keys, 1)
 
     def quant(i, oq, os, sem):
         v.wait_ge(S["lx%d" % i], 16)
         v.quantize_mx(oq, os, T.xb[:, 512 * i:512 * i + 512]).then_inc(sem, 1)
 
-    i = 0
-    for n, group in enumerate(p["groups"]):
-        for q in group:
-            quant(i, T.sq[:, LO * i:LO * i + LO], T.ss[:, LO * i:LO * i + LO], S["qg%d" % n])
-            i += 1
-    v.wait_ge(S.lsc, 16 * 8)
-    v.tensor_copy(T.kin[:, KC * rank:KC * rank + KC], T.sck[:, KC * rank:KC * rank + KC]).then_inc(S.kown, 1)
+    def quant_w(o):
+        v.wait_ge(S["lw%d" % o], 16)
+        v.quantize_mx(T.wq[:, LO * o:LO * o + LO], T.ws[:, LO * o:LO * o + LO],
+                      T.wb[:, 512 * o:512 * o + 512]).then_inc(S["qw%d" % o], 1)
+
+    first = {}
+    for n, call in enumerate(p["calls"]):
+        for kind, owners, _, _ in call:
+            for q in owners:
+                if kind != "k":
+                    first.setdefault(q, n)
+    for i, q in enumerate(order[:N - 1]):
+        quant(i, T.sq[:, LO * i:LO * i + LO], T.ss[:, LO * i:LO * i + LO], S["qc%d" % first[q]])
     mine = LO * (N - 1 - rank)
     quant(N - 1, T.winq[:, mine:mine + LO], T.wins[:, mine:mine + LO], S.qo)
+    v.wait_ge(S.lsc, 32)
+    keys(T.sck[0:KP, KC * rank:KC * rank + KC], rank)
 
-    left = [0]
+    v.wait_ge(S.iot, 2)
+    v.tensor_scalar(T.jp[:, :], T.ip[:, :], 15, None, AluOpType.bitwise_and).then_inc(S.jv, 1)
+    v.wait_ge(S.jv, 1)
+    v.tensor_tensor(T.jt[:, :], T.jp[:, :], T.ic[:, :], AluOpType.add).then_inc(S.jv, 1)
 
-    def send(kind, qs):
+    left = 0
+    g.wait_ge(S.fill, 2)
+    g.wait_ge(S.lsc, 32)
+    for n, call in enumerate(p["calls"]):
+        tiles = list(first.values()).count(n)
+        if tiles:
+            g.wait_ge(S["qc%d" % n], tiles)
         out = []
-        for q in qs:
-            i = order.index(q)
-            far = q in p["relays"]
-            dst = p["relays"][q] if far else T.cores[q]
-            if kind == "k":
-                src = T.sck[:, KC * q:KC * q + KC]
-                to = T.rk[:, :] if far else T.kin[:, KC * rank:KC * rank + KC]
-                rsem = S.rak if far else S.arrk
-            elif kind == "q":
-                src = T.sq[:, LO * i:LO * i + LO].bitcast(dt.uint8)
-                to = (T.rq[:, 0:LO] if far else T.winq[:, mine:mine + LO]).bitcast(dt.uint8)
-                rsem = S.raq if far else S.arrq
+        for hop in call:
+            kind, owners, dst, engines = hop
+            src = piece(T, ("sck", "sq", "ss"), kind, owners[0] if kind == "k" else order.index(owners[0]), len(owners))
+            if dst in T.cores:
+                to, sem = landing(T, topo, kind, rank, owners[0])
             else:
-                src = T.ss[:, LO * i:LO * i + LO]
-                to = T.rs[:, 0:LO] if far else T.wins[:, mine:mine + LO]
-                rsem = S.ras if far else S.arrs
-            e = p["keys" if kind == "k" else "cols"][q]
-            rid, pid = topo.addr(dst, core)
-            out.append(RemoteDMATransfer(dst_ids=[DstId(rid=rid, pnc=pid)], dma_engine_mask=mask_of(e),
-                                         remote_sem=rsem, src=src, dst=to))
-            left[0] += len(e)
+                to, sem = piece(T, ("rk", "rq", "rs"), kind, 0, len(owners)), "ra%d" % steps(p, dst).index(hop)
+            out.append(transfer(topo, core, dst, engines, S[sem], src, to))
+            left += len(engines)
         g.remote_dma_fused(out, local_sem=S.left)
 
-    g.wait_ge(S.lsc, 16 * 8)
-    send("k", order[:N - 1])
-    for n, group in enumerate(p["groups"]):
-        g.wait_ge(S["qg%d" % n], len(group))
-        send("q", group)
-        send("s", group)
-
-    nk = nc = 0
+    arrive = {"arrp": 0, "arrk": 0, "arrl": 0, "arrq": 0, "arrs": 0}
     for r in range(N):
-        if r == rank:
-            continue
-        pr = plan(r, T.cores, topo)
-        if rank in pr["relays"]:
-            e = len(topo.engines(pr["relays"][rank], core))
-            nk, nc = nk + e, nc + e
-        else:
-            nk, nc = nk + len(pr["keys"][rank]), nc + len(pr["cols"][rank])
+        for call in plan(r, T.cores, topo)["calls"]:
+            for kind, owners, dst, engines in call:
+                if rank in owners:
+                    arrive[landing(T, topo, kind, r, rank)[1]] += len(engines if dst == core else topo.engines(dst, core))
 
-    v.wait_ge(S.arrk, nk)
-    v.wait_ge(S.kown, 1)
-    v.tensor_scalar(T.kin8[:, :], T.kin[:, :], N, None, AluOpType.mult).then_inc(S.am, 1)
-    v.wait_ge(S.am, 1)
-    v.tensor_tensor(T.m0[:, :], T.kin8[:, :], T.slot[:, :], AluOpType.add).then_inc(S.am, 1)
-    v.wait_ge(S.am, 2)
-    v.tensor_tensor(T.m1[:, :], T.m0[:, 0:4 * KC], T.m0[:, 4 * KC:8 * KC], AluOpType.max).then_inc(S.am, 1)
-    v.wait_ge(S.am, 3)
-    v.tensor_tensor(T.m2[:, :], T.m1[:, 0:2 * KC], T.m1[:, 2 * KC:4 * KC], AluOpType.max).then_inc(S.am, 1)
-    v.wait_ge(S.am, 4)
-    v.tensor_tensor(T.m3[:, :], T.m2[:, 0:KC], T.m2[:, KC:2 * KC], AluOpType.max).then_inc(S.am, 1)
-    v.wait_ge(S.am, 5)
-    v.tensor_scalar(T.m4[:, :], T.m3[:, :], N - 1, None, AluOpType.bitwise_and).then_inc(S.am, 1)
-    v.wait_ge(S.am, 6)
-    v.wait_ge(S.jv, 3)
-    v.tensor_tensor(T.m5[:, :], T.m4[:, :], T.jf[:, :], AluOpType.add).then_inc(S.am, 1)
-    v.wait_ge(S.am, 7)
-    v.tensor_scalar(T.off[:, :], T.m5[:, :], float(LO), None, AluOpType.mult).then_inc(S.offs, 1)
+    for sem in ("arrp", "arrk", "arrl"):
+        v.wait_ge(S[sem], arrive[sem])
+        for r in range(N):
+            if r != rank and landing(T, topo, "k", r, rank)[1] == sem:
+                keys(T.kin[0:KP, KC * r:KC * r + KC], r)
+    v.wait_ge(S.keys, N)
+    for c in range(KC):
+        v.tensor_reduce(T.m3[0:KP, c:c + 1], T.key[0:KP, c:KC * N:KC], AxisListType.X, AluOpType.max).then_inc(S.am, 1)
+    v.wait_ge(S.am, KC)
+    for h in range(0, 128, KP):
+        v.tensor_scalar(T.m4[h:h + KP, :], T.m3[0:KP, :], N - 1, None, AluOpType.bitwise_and).then_inc(S.am, 1)
+    v.wait_ge(S.am, KC + 128 // KP)
+    v.wait_ge(S.jv, 2)
+    for c in range(KC):
+        v.tensor_scalar(T.off[:, c:c + 1], T.m4[:, c:c + 1], float(LO), T.jt[:, c:c + 1],
+                        AluOpType.mult, AluOpType.add).then_inc(S.offs, 1)
 
-    v.wait_ge(S.lw, 16)
-    v.quantize_mx(T.wq[:, :], T.ws[:, :], T.wb[:, :]).then_inc(S.qw, 1)
-
-    v.wait_ge(S.offs, 1)
+    quant_w(0)
+    v.wait_ge(S.offs, KC)
     v.wait_ge(S.qo, 1)
-    v.wait_ge(S.arrq, nc)
+    v.wait_ge(S.arrq, arrive["arrq"])
     v.tensor_copy(T.mq[:, 0:LO].bitcast(dt.uint32),
                   T.winq[:, 0:NL].bitcast(dt.uint32).indirect(T.off[:, 0:KC])).then_inc(S.pc, 1)
-    sc.wait_ge(S.offs, 1)
+    quant_w(1)
+    sc.wait_ge(S.offs, KC)
     sc.wait_ge(S.qo, 1)
-    sc.wait_ge(S.arrs, nc)
+    sc.wait_ge(S.arrs, arrive["arrs"])
     sc.activation(T.ms[:, 0:LO], T.wins[:, 0:NL].indirect(T.off[:, 0:KC]),
                   ActivationFunctionType.Copy).then_inc(S.pscale, 1)
 
-    te.wait_ge(S.qw, 1)
     te.wait_ge(S.pc, 1)
     te.wait_ge(S.pscale, 1)
     for o, (ps, mm) in enumerate(((T.ps0, S.mm0), (T.ps1, S.mm1))):
+        te.wait_ge(S["qw%d" % o], 1)
         te.matmul_mx(ps[:, 0:LO], T.wq[:, LO * o:LO * o + LO], T.ws[:, LO * o:LO * o + LO], T.mq[:, 0:LO],
                      T.ms[:, 0:LO], True, True).then_inc(mm, 1)
     v.wait_ge(S.mm0, 1)
@@ -229,4 +252,4 @@ def rank_program(g, core, T, topo):
     sc.dma_start(T.y[:, LO:2 * LO], T.ysb[:, LO:2 * LO]).then_inc(S.st1, 16)
     sy.wait_ge(S.st0, 16)
     sc.wait_ge(S.st1, 16)
-    g.wait_ge(S.left, left[0])
+    g.wait_ge(S.left, left)

from concourse.bass import DstId, RemoteDMATransfer
from concourse.mybir import dt, AluOpType, AxisListType, ActivationFunctionType

N, NL, LO, O = 8, 1024, 128, 2
KC = LO // 16
H = N // 2
KP = 32

SCRATCH = {
    "xb": ("sbuf", [128, 4 * NL], "bfloat16"),
    "wb": ("sbuf", [128, 512 * O], "bfloat16"),
    "sck": ("sbuf", [128, KC * N], "int32"),
    "kin": ("sbuf", [128, KC * N], "int32"),
    "key": ("sbuf", [128, KC * N], "float32"),
    "m3": ("sbuf", [128, KC], "int32"),
    "m4": ("sbuf", [128, KC], "int32"),
    "ip": ("sbuf", [128, KC], "int32"),
    "ic": ("sbuf", [128, KC], "int32"),
    "jp": ("sbuf", [128, KC], "int32"),
    "jt": ("sbuf", [128, KC], "float32"),
    "off": ("sbuf", [128, KC], "uint16"),
    "sq": ("sbuf", [128, NL], "float8_e4m3fn_x4"),
    "ss": ("sbuf", [128, NL], "uint8"),
    "rk": ("sbuf", [128, KC], "int32"),
    "rq": ("sbuf", [128, 2 * LO], "float8_e4m3fn_x4"),
    "rs": ("sbuf", [128, 4 * LO], "uint8"),
    "winq": ("sbuf", [128, NL], "float8_e4m3fn_x4"),
    "wins": ("sbuf", [128, NL], "uint8"),
    "mq": ("sbuf", [128, LO], "float8_e4m3fn_x4"),
    "ms": ("sbuf", [128, LO], "uint8"),
    "wq": ("sbuf", [128, LO * O], "float8_e4m3fn_x4"),
    "ws": ("sbuf", [128, LO * O], "uint8"),
    "ps0": ("psum", [128, 512], "float32"),
    "ps1": ("psum", [128, 512], "float32"),
    "ysb": ("sbuf", [128, LO * O], "float32"),
}
SEMAPHORES = (["lsc", "keys", "fill", "lw0", "lw1", "arrp", "iot", "jv", "qo", "qw0", "qw1", "am", "offs", "pc",
               "pscale", "mm0", "mm1", "cp0", "cp1", "st0", "st1", "arrk", "arrl", "arrq", "arrs", "left"]
              + ["lx%d" % i for i in range(N)] + ["qc%d" % i for i in range(N)] + ["ra%d" % i for i in range(4)])


def mask_of(engines):
    return sum(1 << e for e in engines)


def deal(engines, n):
    k = len(engines) // n
    return [engines[k * i:k * i + k] for i in range(n)]


def plan(r, cores, topo):
    me = cores[r]
    chip = [c for c in topo.cores_of(me) if c != me]
    plane = [q for q in range(N) if q == r or topo.same_plane(me, cores[q])]
    cross = [q for q in range(N) if q not in plane]
    i = plane.index(r)
    ports = [c for c in chip if all(topo.may_write(c, cores[q]) for q in cross)]
    near = [c for c in ports if topo.die(c) == topo.die(me)]
    far = [c for c in ports if c not in near]
    helper = [c for c in chip if c not in ports and topo.die(c) != topo.die(me)][0]
    pairs = [(t, t + H) for t in sorted({q % H for q in cross})]
    partner = (r + H) % N
    via = plane[(i + 1) % len(plane)]
    other = (via + H) % N
    out = topo.engines(me, cores[partner])
    on = topo.engines(me, helper)
    stay = [e for e in on if e not in out]
    beside = [c for c in chip if c not in ports and topo.die(c) == topo.die(me)][0]
    ports = near + far

    to = {q: ports[(i + k) % len(ports)] for k, q in enumerate(cross)}
    to.update({via: helper, other: beside, partner: cores[partner]})
    cross = sorted(cross, key=lambda q: to[q] in far)

    def hops(kind, owners, lanes):
        return [(kind, (q,), to[q], e) for q, e in zip(owners, lanes)]

    calls = [hops("k", cross, deal(on, 4)),
             hops("k", [via, other, partner], deal(stay, 2) + [out]),
             hops("q", [partner] + cross, deal(out, 2)[:1] + deal(out, 4)[2:] + deal(stay, 2)),
             hops("s", [partner, via, other] + cross, deal(out, 2)[:1] + deal(out, 4)[2:] + deal(stay, 4)),
             hops("q", [other, via], deal(stay, 2))]
    return {"order": [partner] + cross + [via, other, r], "sides": (sorted(cross), plane), "calls": calls}


def transfer(topo, core, dst, engines, sem, src, to):
    rid, pid = topo.addr(dst, core)
    return RemoteDMATransfer(dst_ids=[DstId(rid=rid, pnc=pid)], dma_engine_mask=mask_of(engines), remote_sem=sem,
                             src=src, dst=to)


def piece(T, names, kind, a, n):
    buf = T[names["kqs".index(kind)]]
    if kind == "k":
        return buf[:, KC * a:KC * a + KC]
    view = buf[:, LO * a:LO * (a + n)]
    return view.bitcast(dt.uint8) if kind == "q" else view


def landing(T, topo, kind, r, q):
    if kind != "k":
        return piece(T, ("kin", "winq", "wins"), kind, N - 1 - r, 1), "arr" + kind
    sem = "arrp" if r % H == q % H else "arrl" if topo.same_plane(T.cores[r], T.cores[q]) else "arrk"
    return piece(T, ("kin",), kind, r, 1), sem


def steps(p, core):
    return [hop for call in p["calls"] for hop in call if hop[2] == core]


def relay_program(g, core, T, topo, r, p):
    S = T.sem
    left = 0
    for n, (kind, owners, _, engines) in enumerate(steps(p, core)):
        g.wait_ge(S["ra%d" % n], len(engines))
        out = topo.engines(core, T.cores[owners[0]])
        to, sem = landing(T, topo, kind, r, owners[0])
        g.remote_dma_fused([transfer(topo, core, T.cores[owners[0]], out, S[sem],
                                     piece(T, ("rk", "rq", "rs"), kind, 0, 1), to)], local_sem=S.left)
        left += len(out)
    if left:
        g.wait_ge(S.left, left)


def rank_program(g, core, T, topo):
    S = T.sem
    rank = T.rank_of(core)
    if rank is None:
        for r in range(N):
            relay_program(g, core, T, topo, r, plan(r, T.cores, topo))
        return

    p = plan(rank, T.cores, topo)
    order = p["order"]
    sy, sc, v, te = g.sync, g.scalar, g.vector, g.tensor

    two = (sy, sc)
    for h in range(2):
        two[h].dma_start(T.sck[16 * h:16 * h + 16, :], T.sc[:, :]).then_inc(S.lsc, 16)
    for i, q in enumerate(order):
        two[i % 2].dma_start(T.xb[:, 512 * i:512 * i + 512], T.x[:, 512 * q:512 * q + 512]).then_inc(S["lx%d" % i], 16)
    sy.wait_ge(S["lx%d" % (N - 2)], 16)
    for o in range(O):
        sy.dma_start(T.wb[:, 512 * o:512 * o + 512], T.w[:, 512 * o:512 * o + 512]).then_inc(S["lw%d" % o], 16)

    g.iota(T.ip[:, :], [[0, KC]], 0, 1).then_inc(S.iot, 1)
    g.iota(T.ic[:, :], [[16, KC]], 0, 0).then_inc(S.iot, 1)

    v.memset(T.sck[32:64, :], 0).then_inc(S.fill, 1)
    v.memset(T.sck[64:128, :], 0).then_inc(S.fill, 1)

    def keys(scores, r):
        v.tensor_scalar(T.key[0:KP, KC * r:KC * r + KC], scores, N, N - 1 - r,
                        AluOpType.mult, AluOpType.add).then_inc(S.keys, 1)

    def quant(i, oq, os, sem):
        v.wait_ge(S["lx%d" % i], 16)
        v.quantize_mx(oq, os, T.xb[:, 512 * i:512 * i + 512]).then_inc(sem, 1)

    def quant_w(o):
        v.wait_ge(S["lw%d" % o], 16)
        v.quantize_mx(T.wq[:, LO * o:LO * o + LO], T.ws[:, LO * o:LO * o + LO],
                      T.wb[:, 512 * o:512 * o + 512]).then_inc(S["qw%d" % o], 1)

    first = {}
    for n, call in enumerate(p["calls"]):
        for kind, owners, _, _ in call:
            for q in owners:
                if kind != "k":
                    first.setdefault(q, n)
    for i, q in enumerate(order[:N - 1]):
        quant(i, T.sq[:, LO * i:LO * i + LO], T.ss[:, LO * i:LO * i + LO], S["qc%d" % first[q]])
    mine = LO * (N - 1 - rank)
    quant(N - 1, T.winq[:, mine:mine + LO], T.wins[:, mine:mine + LO], S.qo)
    v.wait_ge(S.lsc, 32)
    keys(T.sck[0:KP, KC * rank:KC * rank + KC], rank)

    v.wait_ge(S.iot, 2)
    v.tensor_scalar(T.jp[:, :], T.ip[:, :], 15, None, AluOpType.bitwise_and).then_inc(S.jv, 1)
    v.wait_ge(S.jv, 1)
    v.tensor_tensor(T.jt[:, :], T.jp[:, :], T.ic[:, :], AluOpType.add).then_inc(S.jv, 1)

    left = 0
    g.wait_ge(S.fill, 2)
    g.wait_ge(S.lsc, 32)
    for n, call in enumerate(p["calls"]):
        tiles = list(first.values()).count(n)
        if tiles:
            g.wait_ge(S["qc%d" % n], tiles)
        out = []
        for hop in call:
            kind, owners, dst, engines = hop
            src = piece(T, ("sck", "sq", "ss"), kind, owners[0] if kind == "k" else order.index(owners[0]), len(owners))
            if dst in T.cores:
                to, sem = landing(T, topo, kind, rank, owners[0])
            else:
                to, sem = piece(T, ("rk", "rq", "rs"), kind, 0, len(owners)), "ra%d" % steps(p, dst).index(hop)
            out.append(transfer(topo, core, dst, engines, S[sem], src, to))
            left += len(engines)
        g.remote_dma_fused(out, local_sem=S.left)

    arrive = {"arrp": 0, "arrk": 0, "arrl": 0, "arrq": 0, "arrs": 0}
    for r in range(N):
        for call in plan(r, T.cores, topo)["calls"]:
            for kind, owners, dst, engines in call:
                if rank in owners:
                    arrive[landing(T, topo, kind, r, rank)[1]] += len(engines if dst == core else topo.engines(dst, core))

    for sem in ("arrp", "arrk", "arrl"):
        v.wait_ge(S[sem], arrive[sem])
        for r in range(N):
            if r != rank and landing(T, topo, "k", r, rank)[1] == sem:
                keys(T.kin[0:KP, KC * r:KC * r + KC], r)
    v.wait_ge(S.keys, N)
    for c in range(KC):
        v.tensor_reduce(T.m3[0:KP, c:c + 1], T.key[0:KP, c:KC * N:KC], AxisListType.X, AluOpType.max).then_inc(S.am, 1)
    v.wait_ge(S.am, KC)
    for h in range(0, 128, KP):
        v.tensor_scalar(T.m4[h:h + KP, :], T.m3[0:KP, :], N - 1, None, AluOpType.bitwise_and).then_inc(S.am, 1)
    v.wait_ge(S.am, KC + 128 // KP)
    v.wait_ge(S.jv, 2)
    for c in range(KC):
        v.tensor_scalar(T.off[:, c:c + 1], T.m4[:, c:c + 1], float(LO), T.jt[:, c:c + 1],
                        AluOpType.mult, AluOpType.add).then_inc(S.offs, 1)

    quant_w(0)
    v.wait_ge(S.offs, KC)
    v.wait_ge(S.qo, 1)
    v.wait_ge(S.arrq, arrive["arrq"])
    v.tensor_copy(T.mq[:, 0:LO].bitcast(dt.uint32),
                  T.winq[:, 0:NL].bitcast(dt.uint32).indirect(T.off[:, 0:KC])).then_inc(S.pc, 1)
    quant_w(1)
    sc.wait_ge(S.offs, KC)
    sc.wait_ge(S.qo, 1)
    sc.wait_ge(S.arrs, arrive["arrs"])
    sc.activation(T.ms[:, 0:LO], T.wins[:, 0:NL].indirect(T.off[:, 0:KC]),
                  ActivationFunctionType.Copy).then_inc(S.pscale, 1)

    te.wait_ge(S.pc, 1)
    te.wait_ge(S.pscale, 1)
    for o, (ps, mm) in enumerate(((T.ps0, S.mm0), (T.ps1, S.mm1))):
        te.wait_ge(S["qw%d" % o], 1)
        te.matmul_mx(ps[:, 0:LO], T.wq[:, LO * o:LO * o + LO], T.ws[:, LO * o:LO * o + LO], T.mq[:, 0:LO],
                     T.ms[:, 0:LO], True, True).then_inc(mm, 1)
    v.wait_ge(S.mm0, 1)
    v.tensor_copy(T.ysb[:, 0:LO], T.ps0[:, 0:LO]).then_inc(S.cp0, 1)
    sc.wait_ge(S.mm1, 1)
    sc.activation(T.ysb[:, LO:2 * LO], T.ps1[:, 0:LO], ActivationFunctionType.Copy).then_inc(S.cp1, 1)
    sy.wait_ge(S.cp0, 1)
    sy.dma_start(T.y[:, 0:LO], T.ysb[:, 0:LO]).then_inc(S.st0, 16)
    sc.wait_ge(S.cp1, 1)
    sc.dma_start(T.y[:, LO:2 * LO], T.ysb[:, LO:2 * LO]).then_inc(S.st1, 16)
    sy.wait_ge(S.st0, 16)
    sc.wait_ge(S.st1, 16)
    g.wait_ge(S.left, left)
